import numpy as np
import ml_dtypes


def mxq(x, axis, fmt="e4m3"):
    dtype, down = {"e4m3": (ml_dtypes.float8_e4m3fn, 7), "e5m2": (ml_dtypes.float8_e5m2, 14)}[fmt]
    v = np.moveaxis(np.asarray(x, np.float32).astype(ml_dtypes.bfloat16).astype(np.float64), axis, -1)
    blocks = v.reshape(v.shape[:-1] + (-1, 32))
    amax = np.abs(blocks).max(-1, keepdims=True)
    byte = np.maximum(np.where(amax > 0, np.frexp(amax)[1] - 1 + 127, 0) - down, 1)
    scale = np.exp2(byte - 127.0)
    codes = (blocks / scale).astype(np.float32).astype(dtype).astype(np.float64)
    return np.moveaxis((codes * scale).reshape(v.shape), -1, axis)


WIDE = False


def mx_kscale(k):
    if not WIDE:
        return np.ones(k)
    levels = np.array([10, -10, 5, -5, 0])
    if k % 512:
        return np.exp2(np.random.permutation(np.resize(levels, k // 32))).repeat(32)
    a = np.empty((k // 512, 16))
    for p in range(k // 512):
        a[p, :8] = np.random.permutation(np.resize(levels, 8))
        for g in range(8):
            far = levels[np.abs(levels - a[p, g]) >= 10]
            a[p, g + 8] = far[np.random.randint(len(far))]
    return np.exp2(a.ravel()).repeat(32)


def f64(x):
    return np.asarray(x).astype(np.float64)


def striped(idx):
    return np.tile(idx.reshape(-1, 16).T, (8, 1)).astype(np.uint16)


def unstriped(offs):
    return offs[:16].T.reshape(-1).astype(np.int64)


E2M1 = np.array([0.0, 0.5, 1.0, 1.5, 2.0, 3.0, 4.0, 6.0, -0.0, -0.5, -1.0, -1.5, -2.0, -3.0, -4.0, -6.0])


def pack_weight(w, fmt):
    k, n = w.shape
    w = f64(np.asarray(w, np.float32).astype(ml_dtypes.bfloat16)).reshape(k // 32, 32, n)
    amax = np.abs(w).max(1)
    if fmt == "e4m3":
        byte = np.frexp(amax)[1] - 1 + 127 - 7
    else:
        mant, ex = np.frexp(amax / 6.0)
        byte = np.where(mant > 0.5, ex, ex - 1) + 127
    byte = np.clip(np.where(amax > 0, byte, 1), 1, 254)
    scaled = (w * np.exp2(127.0 - byte)[:, None, :]).reshape(k, n).astype(np.float32)
    by_word = np.ascontiguousarray(scaled.reshape(k // 512, 128, 4, n).transpose(0, 1, 3, 2))
    if fmt == "e4m3":
        words = by_word.astype(ml_dtypes.float8_e4m3fn).view(np.uint8)
    else:
        c = by_word.astype(ml_dtypes.float4_e2m1fn).view(np.uint8) & 0xF
        words = (c[..., 0::2] | (c[..., 1::2] << 4)).reshape(k // 512, 128, 2 * n)
    return np.ascontiguousarray(words), np.ascontiguousarray(byte.astype(np.uint8).reshape(k // 512, 16, n))


def unpack_weight(words, scales, fmt):
    g, _, n = scales.shape
    words = np.ascontiguousarray(words).reshape(g, 128, n, -1)
    if fmt == "e4m3":
        vals = words.view(ml_dtypes.float8_e4m3fn).astype(np.float64)
    else:
        nib = np.empty((g, 128, n, 4), np.uint8)
        nib[..., 0::2] = words & 0xF
        nib[..., 1::2] = words >> 4
        vals = E2M1[nib]
    vals = vals * np.repeat(np.exp2(scales.astype(np.float64) - 127.0), 8, axis=1)[..., None]
    return vals.transpose(0, 1, 3, 2).reshape(g * 512, n)


def gelu(v):
    return 0.5 * v * (1.0 + np.tanh(np.sqrt(2.0 / np.pi) * (v + 0.044715 * v**3)))


def striped8(idx):
    return np.concatenate([v.reshape(-1, 16).T for v in idx]).astype(np.uint16)


def unstriped8(offs):
    return np.stack([offs[16 * g:16 * g + 16].T.reshape(-1) for g in range(8)]).astype(np.int64)


def runs(v, idx8):
    k = np.arange(v.shape[0])
    return v[k[:, None], idx8[k % 512 // 64]]


K, T, S, H, P, N = 1536, 4096, 1024, 1024, 512, 768

def setup_inputs():
    n = np.random.standard_normal
    s = mx_kscale(K)[:, None]
    u = mx_kscale(H)[:, None]
    tab_words, tab_scales = pack_weight(n((K, T)) * s, "e4m3")
    w2_words, w2_scales = pack_weight(1.6 * n((H, N)) / np.sqrt(H) / u, "e2m1")
    idx8 = np.stack([np.random.permutation(S)[:P] for _ in range(8)])
    return {
        "tab_words": tab_words, "tab_scales": tab_scales,
        "offs": striped(np.random.permutation(T)[:S]),
        "offs2": striped8(idx8),
        "w1": (0.9 * n((K, H)) / np.sqrt(K) / s).astype(np.float32),
        "limit": np.random.uniform(0.2, 4.0, H).astype(np.float32),
        "temp": np.repeat(np.random.uniform(0.4, 1.6, H // 64), 64).astype(np.float32),
        "mark": (2.5 * n((H, P)) * u).astype(np.float32),
        "gain": (np.random.uniform(0.5, 1.5, H) * u[:, 0]).astype(np.float32),
        "w2_words": w2_words, "w2_scales": w2_scales,
    }

def reference(tab_words, tab_scales, offs, offs2, w1, limit, temp, mark, gain, w2_words, w2_scales):
    v = unpack_weight(tab_words, tab_scales, "e4m3")[:, unstriped(offs)]
    h = np.minimum(mxq(f64(w1), 0, "e4m3").T @ v, f64(limit)[:, None])
    hp = runs(h, unstriped8(offs2))
    top = h.max(axis=1)
    a = np.exp(f64(temp)[:, None] * (hp - top[:, None]))
    z = np.maximum(f64(mark) * a, f64(gain)[:, None] * hp)
    w2 = unpack_weight(w2_words, w2_scales, "e2m1")
    return np.tanh(w2.T @ mxq(z, 0, "e4m3"))

@@ -1,0 +1,262 @@
+from contextlib import ExitStack
+
+import concourse.mybir as mybir
+
+K, T, S, H, M, N = 1536, 4096, 1024, 1024, 512, 768
+FLOPS = 2 * K * H * S + 2 * H * N * M
+
+F32 = mybir.dt.float32
+BF16 = mybir.dt.bfloat16
+I32 = mybir.dt.int32
+U32 = mybir.dt.uint32
+U16 = mybir.dt.uint16
+U8 = mybir.dt.uint8
+FP8X4 = mybir.dt.float8_e4m3fn_x4
+FP4X4 = mybir.dt.float4_e2m1fn_x4
+ALU = mybir.AluOpType
+ACT = mybir.ActivationFunctionType
+
+P = 128
+PACK = 4
+K_PASS = P * PACK
+BANK = 512
+K_PASSES = K // K_PASS
+R_PASSES = H // K_PASS
+HALF = M // 2
+VECTOR_SHARE = (88, 48)
+
+
+def tile_list_brush_wear_profile_kernel(
+    tc, tab_words, tab_scales, offs, offs2, w1, limit, temp, mark, gain, w2_words, w2_scales, out
+):
+    nc = tc.nc
+    with ExitStack() as ctx:
+        keep = ctx.enter_context(tc.tile_pool(name="keep", bufs=1))
+        ring = ctx.enter_context(tc.tile_pool(name="ring", bufs=2))
+        psum = ctx.enter_context(tc.psum_pool(name="psum", bufs=1))
+
+        def bank(index):
+            return psum.tile([P, BANK], F32, name="bank%d" % index)
+
+        picks = keep.tile([P, S // 16], U16, name="picks")
+        looks = keep.tile([P, M // 16], U16, name="looks")
+        table = [keep.tile([P, T], I32, name="table%d" % a) for a in range(K_PASSES)]
+        table_scales = keep.tile([P, T], U8, name="table_scales")
+        w2_codes = keep.tile([P, R_PASSES, 2 * N], U8, name="w2_codes", align_bytes=64)
+        w2_planes = keep.tile([P, R_PASSES, N], U8, name="w2_planes", align_bytes=64)
+        marks = [keep.tile([P, PACK, M], F32, name="mark%d" % b) for b in range(R_PASSES)]
+        rows = {}
+        for name in ("limit", "temp", "gain", "minus_temp", "bias"):
+            rows[name] = keep.tile([P, R_PASSES * PACK], F32, name=name)
+        bank_tops = keep.tile([P, 2 * R_PASSES * PACK], F32, name="bank_tops")
+
+        nc.vector.memset(table_scales[:].bitcast(I32), 0)
+        nc.vector.memset(w2_planes[:].rearrange("p a n -> p (a n)").bitcast(I32), 0)
+        for name, vec in (("limit", limit), ("temp", temp), ("gain", gain)):
+            nc.gpsimd.dma_start(
+                out=rows[name][:].rearrange("p (b i) -> p b i", i=PACK),
+                in_=vec.rearrange("(b p i) -> p b i", p=P, i=PACK),
+            )
+
+        w1_raw = {}
+
+        def load_table(a):
+            nc.sync.dma_start(out=table[a][:], in_=tab_words[a].rearrange("p t i -> p (t i)").bitcast(I32))
+
+        def load_w1(b, a):
+            raw = ring.tile([P, PACK, K_PASS], F32, name="w1_raw", bufs=4)
+            src = w1[K_PASS * a : K_PASS * (a + 1), K_PASS * b : K_PASS * (b + 1)]
+            nc.sync.dma_start(out=raw[:], in_=src.rearrange("(p j) c -> p j c", j=PACK))
+            w1_raw[(b, a)] = raw
+
+        def load_mark(b):
+            src = mark[K_PASS * b : K_PASS * (b + 1), :]
+            nc.sync.dma_start(out=marks[b][:], in_=src.rearrange("(p i) m -> p i m", i=PACK))
+
+        picked = [keep.tile([P, S], U32, name="picked%d" % a, align_bytes=64) for a in range(K_PASSES)]
+        picked_scales = keep.tile([P, S], U8, name="picked_scales", align_bytes=64)
+        w1_codes = {}
+        w1_planes = {}
+        w1_grouped = {}
+
+        def round_w1(b, a):
+            grouped = ring.tile([P, PACK * K_PASS], BF16, name="w1_grouped", bufs=3, align_bytes=64)
+            dst = grouped[:].rearrange("p (t m j) -> p m j t", t=PACK, j=PACK)
+            src = w1_raw[(b, a)][:].rearrange("p j (m t) -> p m j t", t=PACK)
+            cut = VECTOR_SHARE[b]
+            nc.vector.tensor_copy(out=dst[:, :cut], in_=src[:, :cut])
+            nc.scalar.copy(out=dst[:, cut:], in_=src[:, cut:])
+            w1_grouped[(b, a)] = grouped
+
+        def quantise_w1(b, a):
+            codes = keep.tile([P, K_PASS], U32, name="w1_codes%d%d" % (b, a), align_bytes=64)
+            plane = keep.tile([P, K_PASS], U8, name="w1_plane%d%d" % (b, a), align_bytes=64)
+            nc.vector.quantize_mx(out=codes[:].bitcast(FP8X4), scales=plane[:], in_=w1_grouped[(b, a)][:])
+            w1_codes[(b, a)] = codes
+            w1_planes[(b, a)] = plane
+
+        def first_pass(acc, b, i, c, a):
+            stat = slice(P * i, P * (i + 1))
+            cols = slice(BANK * c, BANK * (c + 1))
+            nc.tensor.matmul_mx(
+                out=acc[:],
+                lhsT=w1_codes[(b, a)][:, stat].bitcast(FP8X4),
+                lhsT_scale=w1_planes[(b, a)][:, stat],
+                rhs=picked[a][:, cols].bitcast(FP8X4),
+                rhs_scale=picked_scales[4 * a :, cols],
+                start=(a == 0),
+                stop=(a == K_PASSES - 1),
+            )
+
+        scores = {}
+
+        def clip_scores(b, i, accs):
+            k = PACK * b + i
+            h = ring.tile([P, S], F32, name="h", bufs=5)
+            for c in range(2):
+                nc.vector.tensor_scalar(
+                    out=h[:, BANK * c : BANK * (c + 1)],
+                    in0=accs[c][:],
+                    scalar1=rows["limit"][:, k : k + 1],
+                    scalar2=None,
+                    op0=ALU.min,
+                    op1=ALU.max,
+                    accum_out=bank_tops[:, 2 * k + c : 2 * k + c + 1],
+                )
+            nc.vector.tensor_scalar(
+                out=rows["bias"][:, k : k + 1],
+                in0=bank_tops[:, 2 * k : 2 * k + 1],
+                scalar1=bank_tops[:, 2 * k + 1 : 2 * k + 2],
+                scalar2=rows["minus_temp"][:, k : k + 1],
+                op0=ALU.max,
+                op1=ALU.mult,
+            )
+            scores[(b, i)] = h
+
+        def look(b, i, m0, width, z_planes):
+            k = PACK * b + i
+            entries = looks[:, m0 // 16 : (m0 + width) // 16]
+            h = scores[(b, i)]
+            below = ring.tile([P, width], F32, name="below", bufs=4)
+            plain = ring.tile([P, width], F32, name="plain", bufs=4)
+            marked = ring.tile([P, width], F32, name="marked", bufs=3)
+            nc.scalar.activation(
+                out=below[:],
+                in_=h[:].indirect(entries),
+                func=ACT.Exp,
+                bias=rows["bias"][:, k : k + 1],
+                scale=rows["temp"][:, k : k + 1],
+            )
+            nc.scalar.activation(out=plain[:], in_=h[:].indirect(entries), func=ACT.Copy)
+            nc.vector.tensor_tensor(out=marked[:], in0=below[:], in1=marks[b][:, i, m0 : m0 + width], op=ALU.mult)
+            nc.vector.scalar_tensor_tensor(
+                out=z_planes[:, i, :],
+                in0=plain[:],
+                scalar=rows["gain"][:, k : k + 1],
+                in1=marked[:],
+                op0=ALU.mult,
+                op1=ALU.max,
+            )
+
+        z_codes = [keep.tile([P, M], U32, name="z_codes%d" % b, align_bytes=64) for b in range(R_PASSES)]
+        z_scales = [keep.tile([P, M], U8, name="z_scales%d" % b, align_bytes=64) for b in range(R_PASSES)]
+
+        def make_z(b, m0, width):
+            z_planes = ring.tile([P, PACK, width], BF16, name="z_planes")
+            for i in range(PACK):
+                look(b, i, m0, width, z_planes)
+            grouped = ring.tile([P, PACK * width], BF16, name="z_grouped", align_bytes=64)
+            nc.vector.tensor_copy(
+                out=grouped[:].rearrange("p (c u i) -> p c i u", u=4, i=PACK),
+                in_=z_planes[:].rearrange("p i (c u) -> p c i u", u=4),
+            )
+            nc.vector.quantize_mx(
+                out=z_codes[b][:, m0 : m0 + width].bitcast(FP8X4),
+                scales=z_scales[b][:, m0 : m0 + width],
+                in_=grouped[:],
+            )
+
+        def second_pass(acc, pair, m0, b):
+            cols = slice(m0, m0 + HALF)
+            for u in range(2):
+                n0 = P * (2 * pair + u)
+                nc.tensor.matmul_mx(
+                    out=acc[:, HALF * u : HALF * (u + 1)],
+                    lhsT=w2_codes[:, b, 2 * n0 : 2 * (n0 + P)].bitcast(FP4X4),
+                    lhsT_scale=w2_planes[:, b, n0 : n0 + P],
+                    rhs=z_codes[b][:, cols].bitcast(FP8X4),
+                    rhs_scale=z_scales[b][:, cols],
+                    start=(b == 0 and u == 0),
+                    stop=(b == R_PASSES - 1 and u == 1),
+                )
+
+        def finish(acc, pair, m0):
+            result = ring.tile([P, BANK], F32, name="result", bufs=6)
+            nc.scalar.activation(out=result[:], in_=acc[:], func=ACT.Tanh)
+            dst = out[2 * P * pair : 2 * P * (pair + 1), m0 : m0 + HALF]
+            nc.sync.dma_start(
+                out=dst.rearrange("(u p) m -> p u m", p=P),
+                in_=result[:].rearrange("p (u m) -> p u m", u=2),
+            )
+
+        nc.sync.dma_start(picks[:], offs)
+        for a in range(K_PASSES):
+            load_table(a)
+            load_w1(0, a)
+            if a == 0:
+                for q in range(4):
+                    nc.sync.dma_start(
+                        out=table_scales[32 * q : 32 * q + 4 * K_PASSES, :].bitcast(I32),
+                        in_=tab_scales[:, 4 * q : 4 * q + 4, :].bitcast(I32),
+                    )
+        nc.sync.dma_start(looks[:], offs2)
+        load_w1(1, 0)
+        load_mark(0)
+
+        nc.vector.tensor_scalar(
+            out=rows["minus_temp"][:], in0=rows["temp"][:], scalar1=-1.0, scalar2=None, op0=ALU.mult
+        )
+        nc.vector.tensor_copy(out=picked_scales[:], in_=table_scales[:].indirect(picks[:]))
+        accs = [[bank(2 * i + c) for c in range(2)] for i in range(PACK)]
+        for a in range(K_PASSES):
+            nc.vector.tensor_copy(out=picked[a][:], in_=table[a][:].bitcast(U32).indirect(picks[:]))
+            round_w1(0, a)
+            quantise_w1(0, a)
+            for i in range(PACK):
+                for c in range(2):
+                    first_pass(accs[i][c], 0, i, c, a)
+
+        load_w1(1, 1)
+        load_w1(1, 2)
+        load_mark(1)
+        nc.sync.dma_start(
+            out=w2_codes[:].bitcast(I32), in_=w2_words.bitcast(I32).rearrange("a p n -> p a n")
+        )
+        for q in range(4):
+            nc.sync.dma_start(
+                out=w2_planes[32 * q : 32 * q + 4].bitcast(I32),
+                in_=w2_scales[:, 4 * q : 4 * q + 4, :].bitcast(I32).rearrange("a r n -> r a n"),
+            )
+
+        for i in range(PACK):
+            clip_scores(0, i, accs[i])
+        for a in range(K_PASSES):
+            round_w1(1, a)
+            quantise_w1(1, a)
+        make_z(0, 0, M)
+
+        accs = [[bank(2 * i + c) for c in range(2)] for i in range(PACK)]
+        for i in range(PACK):
+            for c in range(2):
+                for a in range(K_PASSES):
+                    first_pass(accs[i][c], 1, i, c, a)
+            clip_scores(1, i, accs[i])
+
+        for half in range(2):
+            outs = [bank(3 * half + pair) for pair in range(3)]
+            for pair in range(3):
+                second_pass(outs[pair], pair, HALF * half, 0)
+            make_z(1, HALF * half, HALF)
+            for pair in range(3):
+                second_pass(outs[pair], pair, HALF * half, 1)
+                finish(outs[pair], pair, HALF * half)

@@ -23,7 +23,7 @@ BANK = 512
 K_PASSES = K // K_PASS
 R_PASSES = H // K_PASS
 HALF = M // 2
-VECTOR_SHARE = (88, 48)
+VECTOR_SHARE = (88, 24)
 
 
 def tile_list_brush_wear_profile_kernel(
@@ -40,7 +40,7 @@ def tile_list_brush_wear_profile_kernel(
 
         picks = keep.tile([P, S // 16], U16, name="picks")
         looks = keep.tile([P, M // 16], U16, name="looks")
-        table = [keep.tile([P, T], I32, name="table%d" % a) for a in range(K_PASSES)]
+        table = [keep.tile([P, T], I32, name="table%d" % a, tag="table%d" % a) for a in range(K_PASSES)]
         table_scales = keep.tile([P, T], U8, name="table_scales")
         w2_codes = keep.tile([P, R_PASSES, 2 * N], U8, name="w2_codes", align_bytes=64)
         w2_planes = keep.tile([P, R_PASSES, N], U8, name="w2_planes", align_bytes=64)
@@ -64,7 +64,7 @@ def tile_list_brush_wear_profile_kernel(
             nc.sync.dma_start(out=table[a][:], in_=tab_words[a].rearrange("p t i -> p (t i)").bitcast(I32))
 
         def load_w1(b, a):
-            raw = ring.tile([P, PACK, K_PASS], F32, name="w1_raw", bufs=4)
+            raw = ring.tile([P, PACK, K_PASS], F32, name="w1_raw", bufs=3)
             src = w1[K_PASS * a : K_PASS * (a + 1), K_PASS * b : K_PASS * (b + 1)]
             nc.sync.dma_start(out=raw[:], in_=src.rearrange("(p j) c -> p j c", j=PACK))
             w1_raw[(b, a)] = raw
@@ -81,8 +81,8 @@ def tile_list_brush_wear_profile_kernel(
 
         def round_w1(b, a):
             grouped = ring.tile([P, PACK * K_PASS], BF16, name="w1_grouped", bufs=3, align_bytes=64)
-            dst = grouped[:].rearrange("p (t m j) -> p m j t", t=PACK, j=PACK)
-            src = w1_raw[(b, a)][:].rearrange("p j (m t) -> p m j t", t=PACK)
+            dst = grouped[:].rearrange("p (t m j) -> p m t j", t=PACK, j=PACK)
+            src = w1_raw[(b, a)][:].rearrange("p j (m t) -> p m t j", t=PACK)
             cut = VECTOR_SHARE[b]
             nc.vector.tensor_copy(out=dst[:, :cut], in_=src[:, :cut])
             nc.scalar.copy(out=dst[:, cut:], in_=src[:, cut:])
@@ -112,7 +112,7 @@ def tile_list_brush_wear_profile_kernel(
 
         def clip_scores(b, i, accs):
             k = PACK * b + i
-            h = ring.tile([P, S], F32, name="h", bufs=5)
+            h = keep.tile([P, S], F32, name="h%d" % k)
             for c in range(2):
                 nc.vector.tensor_scalar(
                     out=h[:, BANK * c : BANK * (c + 1)],
@@ -133,38 +133,49 @@ def tile_list_brush_wear_profile_kernel(
             )
             scores[(b, i)] = h
 
-        def look(b, i, m0, width, z_planes):
-            k = PACK * b + i
+        below = {}
+        plain = {}
+
+        def look(b, m0, width):
             entries = looks[:, m0 // 16 : (m0 + width) // 16]
-            h = scores[(b, i)]
-            below = ring.tile([P, width], F32, name="below", bufs=4)
-            plain = ring.tile([P, width], F32, name="plain", bufs=4)
-            marked = ring.tile([P, width], F32, name="marked", bufs=3)
-            nc.scalar.activation(
-                out=below[:],
-                in_=h[:].indirect(entries),
-                func=ACT.Exp,
-                bias=rows["bias"][:, k : k + 1],
-                scale=rows["temp"][:, k : k + 1],
-            )
-            nc.scalar.activation(out=plain[:], in_=h[:].indirect(entries), func=ACT.Copy)
-            nc.vector.tensor_tensor(out=marked[:], in0=below[:], in1=marks[b][:, i, m0 : m0 + width], op=ALU.mult)
-            nc.vector.scalar_tensor_tensor(
-                out=z_planes[:, i, :],
-                in0=plain[:],
-                scalar=rows["gain"][:, k : k + 1],
-                in1=marked[:],
-                op0=ALU.mult,
-                op1=ALU.max,
-            )
+            below[(b, m0)] = keep.tile([P, PACK, width], F32, name="below%d_%d" % (b, m0))
+            plain[(b, m0)] = keep.tile([P, PACK, width], F32, name="plain%d_%d" % (b, m0))
+            for i in range(PACK):
+                k = PACK * b + i
+                h = scores[(b, i)]
+                nc.scalar.activation(
+                    out=below[(b, m0)][:, i, :],
+                    in_=h[:].indirect(entries),
+                    func=ACT.Exp,
+                    bias=rows["bias"][:, k : k + 1],
+                    scale=rows["temp"][:, k : k + 1],
+                )
+                nc.scalar.activation(out=plain[(b, m0)][:, i, :], in_=h[:].indirect(entries), func=ACT.Copy)
 
         z_codes = [keep.tile([P, M], U32, name="z_codes%d" % b, align_bytes=64) for b in range(R_PASSES)]
         z_scales = [keep.tile([P, M], U8, name="z_scales%d" % b, align_bytes=64) for b in range(R_PASSES)]
 
         def make_z(b, m0, width):
             z_planes = ring.tile([P, PACK, width], BF16, name="z_planes")
-            for i in range(PACK):
-                look(b, i, m0, width, z_planes)
+            step = M // width
+            for i0 in range(0, PACK, step):
+                marked = ring.tile([P, step, width], F32, name="marked", bufs=3)
+                nc.vector.tensor_tensor(
+                    out=marked[:],
+                    in0=below[(b, m0)][:, i0 : i0 + step, :],
+                    in1=marks[b][:, i0 : i0 + step, m0 : m0 + width],
+                    op=ALU.mult,
+                )
+                for i in range(i0, i0 + step):
+                    k = PACK * b + i
+                    nc.vector.scalar_tensor_tensor(
+                        out=z_planes[:, i, :],
+                        in0=plain[(b, m0)][:, i, :],
+                        scalar=rows["gain"][:, k : k + 1],
+                        in1=marked[:, i - i0, :],
+                        op0=ALU.mult,
+                        op1=ALU.max,
+                    )
             grouped = ring.tile([P, PACK * width], BF16, name="z_grouped", align_bytes=64)
             nc.vector.tensor_copy(
                 out=grouped[:].rearrange("p (c u i) -> p c i u", u=4, i=PACK),
@@ -191,12 +202,12 @@ def tile_list_brush_wear_profile_kernel(
                 )
 
         def finish(acc, pair, m0):
-            result = ring.tile([P, BANK], F32, name="result", bufs=6)
-            nc.scalar.activation(out=result[:], in_=acc[:], func=ACT.Tanh)
+            result = results[pair][:, m0 // HALF, :]
+            nc.scalar.activation(out=result, in_=acc[:], func=ACT.Tanh)
             dst = out[2 * P * pair : 2 * P * (pair + 1), m0 : m0 + HALF]
             nc.sync.dma_start(
                 out=dst.rearrange("(u p) m -> p u m", p=P),
-                in_=result[:].rearrange("p (u m) -> p u m", u=2),
+                in_=result.rearrange("p (u m) -> p u m", u=2),
             )
 
         nc.sync.dma_start(picks[:], offs)
@@ -210,8 +221,6 @@ def tile_list_brush_wear_profile_kernel(
                         in_=tab_scales[:, 4 * q : 4 * q + 4, :].bitcast(I32),
                     )
         nc.sync.dma_start(looks[:], offs2)
-        load_w1(1, 0)
-        load_mark(0)
 
         nc.vector.tensor_scalar(
             out=rows["minus_temp"][:], in0=rows["temp"][:], scalar1=-1.0, scalar2=None, op0=ALU.mult
@@ -226,8 +235,10 @@ def tile_list_brush_wear_profile_kernel(
                 for c in range(2):
                     first_pass(accs[i][c], 0, i, c, a)
 
+        load_w1(1, 0)
         load_w1(1, 1)
         load_w1(1, 2)
+        load_mark(0)
         load_mark(1)
         nc.sync.dma_start(
             out=w2_codes[:].bitcast(I32), in_=w2_words.bitcast(I32).rearrange("a p n -> p a n")
@@ -243,7 +254,7 @@ def tile_list_brush_wear_profile_kernel(
         for a in range(K_PASSES):
             round_w1(1, a)
             quantise_w1(1, a)
-        make_z(0, 0, M)
+        look(0, 0, M)
 
         accs = [[bank(2 * i + c) for c in range(2)] for i in range(PACK)]
         for i in range(PACK):
@@ -251,7 +262,11 @@ def tile_list_brush_wear_profile_kernel(
                 for a in range(K_PASSES):
                     first_pass(accs[i][c], 1, i, c, a)
             clip_scores(1, i, accs[i])
+        make_z(0, 0, M)
+        for half in range(2):
+            look(1, HALF * half, HALF)
 
+        results = [keep.tile([P, 2, BANK], F32, name="result%d" % pair, tag="table%d" % pair) for pair in range(3)]
         for half in range(2):
             outs = [bank(3 * half + pair) for pair in range(3)]
             for pair in range(3):

@@ -23,7 +23,7 @@ BANK = 512
 K_PASSES = K // K_PASS
 R_PASSES = H // K_PASS
 HALF = M // 2
-VECTOR_SHARE = (88, 24)
+VECTOR_SLOTS = ((3, 3, 3), (0, 4, 0))
 
 
 def tile_list_brush_wear_profile_kernel(
@@ -44,18 +44,26 @@ def tile_list_brush_wear_profile_kernel(
         table_scales = keep.tile([P, T], U8, name="table_scales")
         w2_codes = keep.tile([P, R_PASSES, 2 * N], U8, name="w2_codes", align_bytes=64)
         w2_planes = keep.tile([P, R_PASSES, N], U8, name="w2_planes", align_bytes=64)
-        marks = [keep.tile([P, PACK, M], F32, name="mark%d" % b) for b in range(R_PASSES)]
+        marks = {}
         rows = {}
         for name in ("limit", "temp", "gain", "minus_temp", "bias"):
-            rows[name] = keep.tile([P, R_PASSES * PACK], F32, name=name)
-        bank_tops = keep.tile([P, 2 * R_PASSES * PACK], F32, name="bank_tops")
+            for b in range(R_PASSES):
+                rows[(name, b)] = keep.tile([P, PACK], F32, name="%s%d" % (name, b), tag="%s%d" % (name, b))
+        bank_tops = [
+            keep.tile([P, 2 * PACK], F32, name="bank_tops%d" % b, tag="bank_tops%d" % b, align_bytes=64)
+            for b in range(R_PASSES)
+        ]
 
         nc.vector.memset(table_scales[:].bitcast(I32), 0)
         nc.vector.memset(w2_planes[:].rearrange("p a n -> p (a n)").bitcast(I32), 0)
-        for name, vec in (("limit", limit), ("temp", temp), ("gain", gain)):
-            nc.gpsimd.dma_start(
-                out=rows[name][:].rearrange("p (b i) -> p b i", i=PACK),
-                in_=vec.rearrange("(b p i) -> p b i", p=P, i=PACK),
+
+        def load_rows(queue, name, vec, b):
+            src = vec[K_PASS * b : K_PASS * (b + 1)]
+            queue.dma_start(out=rows[(name, b)][:], in_=src.rearrange("(p i) -> p i", i=PACK))
+
+        def negate_temp(b):
+            nc.vector.tensor_scalar(
+                out=rows[("minus_temp", b)][:], in0=rows[("temp", b)][:], scalar1=-1.0, scalar2=None, op0=ALU.mult
             )
 
         w1_raw = {}
@@ -64,12 +72,20 @@ def tile_list_brush_wear_profile_kernel(
             nc.sync.dma_start(out=table[a][:], in_=tab_words[a].rearrange("p t i -> p (t i)").bitcast(I32))
 
         def load_w1(b, a):
-            raw = ring.tile([P, PACK, K_PASS], F32, name="w1_raw", bufs=3)
+            raw = keep.tile([P, PACK, K_PASS], F32, name="w1_raw%d%d" % (b, a), tag="w1_raw%d%d" % (b, a))
             src = w1[K_PASS * a : K_PASS * (a + 1), K_PASS * b : K_PASS * (b + 1)]
-            nc.sync.dma_start(out=raw[:], in_=src.rearrange("(p j) c -> p j c", j=PACK))
+            src = src.rearrange("(p j) c -> p j c", j=PACK)
+            for js in row_pieces(b, a):
+                nc.sync.dma_start(out=raw[:, js, :], in_=src[:, js, :])
             w1_raw[(b, a)] = raw
 
+        def row_pieces(b, a):
+            if (b, a) == (0, K_PASSES - 1):
+                return [slice(0, 2), slice(2, 4)]
+            return [slice(0, PACK)]
+
         def load_mark(b):
+            marks[b] = keep.tile([P, PACK, M], F32, name="mark%d" % b, tag="w1_raw0%d" % b)
             src = mark[K_PASS * b : K_PASS * (b + 1), :]
             nc.sync.dma_start(out=marks[b][:], in_=src.rearrange("(p i) m -> p i m", i=PACK))
 
@@ -80,18 +96,32 @@ def tile_list_brush_wear_profile_kernel(
         w1_grouped = {}
 
         def round_w1(b, a):
-            grouped = ring.tile([P, PACK * K_PASS], BF16, name="w1_grouped", bufs=3, align_bytes=64)
+            if (b, a) == (1, 1):
+                grouped = keep.tile([P, PACK * K_PASS], BF16, name="w1_late", tag="h2", align_bytes=64)
+            elif (b, a) == (1, 2):
+                grouped = keep.tile([P, PACK * K_PASS], BF16, name="w1_last", tag="w1_grouped12", align_bytes=64)
+            else:
+                grouped = ring.tile([P, PACK * K_PASS], BF16, name="w1_grouped", align_bytes=64)
             dst = grouped[:].rearrange("p (t m j) -> p m t j", t=PACK, j=PACK)
             src = w1_raw[(b, a)][:].rearrange("p j (m t) -> p m t j", t=PACK)
-            cut = VECTOR_SHARE[b]
-            nc.vector.tensor_copy(out=dst[:, :cut], in_=src[:, :cut])
-            nc.scalar.copy(out=dst[:, cut:], in_=src[:, cut:])
+            cut = VECTOR_SLOTS[b][a]
+            for js in row_pieces(b, a):
+                if cut:
+                    nc.vector.tensor_copy(out=dst[:, :, :cut, js], in_=src[:, :, :cut, js])
+                if cut < PACK:
+                    nc.scalar.copy(out=dst[:, :, cut:, js], in_=src[:, :, cut:, js])
             w1_grouped[(b, a)] = grouped
 
         def quantise_w1(b, a):
             codes = keep.tile([P, K_PASS], U32, name="w1_codes%d%d" % (b, a), align_bytes=64)
             plane = keep.tile([P, K_PASS], U8, name="w1_plane%d%d" % (b, a), align_bytes=64)
-            nc.vector.quantize_mx(out=codes[:].bitcast(FP8X4), scales=plane[:], in_=w1_grouped[(b, a)][:])
+            width = P if (b, a) == (0, K_PASSES - 1) else K_PASS
+            for c0 in range(0, K_PASS, width):
+                nc.vector.quantize_mx(
+                    out=codes[:, c0 : c0 + width].bitcast(FP8X4),
+                    scales=plane[:, c0 : c0 + width],
+                    in_=w1_grouped[(b, a)][:, PACK * c0 : PACK * (c0 + width)],
+                )
             w1_codes[(b, a)] = codes
             w1_planes[(b, a)] = plane
 
@@ -112,67 +142,78 @@ def tile_list_brush_wear_profile_kernel(
 
         def clip_scores(b, i, accs):
             k = PACK * b + i
-            h = keep.tile([P, S], F32, name="h%d" % k)
+            h = keep.tile([P, S], F32, name="h%d" % k, tag="h%d" % k, align_bytes=64)
             for c in range(2):
                 nc.vector.tensor_scalar(
                     out=h[:, BANK * c : BANK * (c + 1)],
                     in0=accs[c][:],
-                    scalar1=rows["limit"][:, k : k + 1],
+                    scalar1=rows[("limit", b)][:, i : i + 1],
                     scalar2=None,
                     op0=ALU.min,
                     op1=ALU.max,
-                    accum_out=bank_tops[:, 2 * k + c : 2 * k + c + 1],
+                    accum_out=bank_tops[b][:, 2 * i + c : 2 * i + c + 1],
                 )
-            nc.vector.tensor_scalar(
-                out=rows["bias"][:, k : k + 1],
-                in0=bank_tops[:, 2 * k : 2 * k + 1],
-                scalar1=bank_tops[:, 2 * k + 1 : 2 * k + 2],
-                scalar2=rows["minus_temp"][:, k : k + 1],
+            nc.gpsimd.tensor_scalar(
+                out=rows[("bias", b)][:, i : i + 1],
+                in0=bank_tops[b][:, 2 * i : 2 * i + 1],
+                scalar1=bank_tops[b][:, 2 * i + 1 : 2 * i + 2],
+                scalar2=rows[("minus_temp", b)][:, i : i + 1],
                 op0=ALU.max,
                 op1=ALU.mult,
             )
             scores[(b, i)] = h
 
-        below = {}
-        plain = {}
+        found = {}
+
+        def slot_groups(b):
+            return [(0, 1), (1, PACK)] if b == 0 else [(0, 2), (2, PACK)]
 
         def look(b, m0, width):
             entries = looks[:, m0 // 16 : (m0 + width) // 16]
-            below[(b, m0)] = keep.tile([P, PACK, width], F32, name="below%d_%d" % (b, m0))
-            plain[(b, m0)] = keep.tile([P, PACK, width], F32, name="plain%d_%d" % (b, m0))
-            for i in range(PACK):
-                k = PACK * b + i
-                h = scores[(b, i)]
-                nc.scalar.activation(
-                    out=below[(b, m0)][:, i, :],
-                    in_=h[:].indirect(entries),
-                    func=ACT.Exp,
-                    bias=rows["bias"][:, k : k + 1],
-                    scale=rows["temp"][:, k : k + 1],
-                )
-                nc.scalar.activation(out=plain[(b, m0)][:, i, :], in_=h[:].indirect(entries), func=ACT.Copy)
+            for i0, i1 in slot_groups(b):
+                below_tag = ("w1_raw12" if i0 else "w1_raw10") if b == 0 else "below%d_%d" % (m0, i0)
+                plain_tag = "table%d" % i0 if b == 0 else "plain%d_%d" % (m0, i0)
+                below = keep.tile([P, i1 - i0, width], F32, name="below", tag=below_tag)
+                plain = keep.tile([P, i1 - i0, width], F32, name="plain", tag=plain_tag)
+                for i in range(i0, i1):
+                    h = scores[(b, i)]
+                    nc.scalar.activation(
+                        out=below[:, i - i0, :],
+                        in_=h[:].indirect(entries),
+                        func=ACT.Exp,
+                        bias=rows[("bias", b)][:, i : i + 1],
+                        scale=rows[("temp", b)][:, i : i + 1],
+                    )
+                    nc.scalar.activation(out=plain[:, i - i0, :], in_=h[:].indirect(entries), func=ACT.Copy)
+                found[(b, m0, i0)] = (below, plain)
 
         z_codes = [keep.tile([P, M], U32, name="z_codes%d" % b, align_bytes=64) for b in range(R_PASSES)]
         z_scales = [keep.tile([P, M], U8, name="z_scales%d" % b, align_bytes=64) for b in range(R_PASSES)]
 
         def make_z(b, m0, width):
-            z_planes = ring.tile([P, PACK, width], BF16, name="z_planes")
-            step = M // width
-            for i0 in range(0, PACK, step):
-                marked = ring.tile([P, step, width], F32, name="marked", bufs=3)
-                nc.vector.tensor_tensor(
-                    out=marked[:],
-                    in0=below[(b, m0)][:, i0 : i0 + step, :],
-                    in1=marks[b][:, i0 : i0 + step, m0 : m0 + width],
-                    op=ALU.mult,
-                )
-                for i in range(i0, i0 + step):
-                    k = PACK * b + i
+            if b == 0:
+                z_planes = keep.tile([P, PACK, width], BF16, name="z_planes0", tag="limit1")
+                marked = keep.tile([P, PACK, width], F32, name="marked0", tag="w1_grouped12", align_bytes=64)
+            else:
+                z_planes = ring.tile([P, PACK, width], BF16, name="z_planes")
+                marked = ring.tile([P, PACK, width], F32, name="marked")
+            for i0, i1 in slot_groups(b):
+                below, plain = found[(b, m0, i0)]
+                if b == 0:
+                    for i in range(i0, i1):
+                        nc.gpsimd.tensor_tensor(
+                            out=marked[:, i, :], in0=below[:, i - i0, :], in1=marks[b][:, i, :], op=ALU.mult
+                        )
+                else:
+                    nc.vector.tensor_tensor(
+                        out=marked[:, i0:i1, :], in0=below[:], in1=marks[b][:, i0:i1, m0 : m0 + width], op=ALU.mult
+                    )
+                for i in range(i0, i1):
                     nc.vector.scalar_tensor_tensor(
                         out=z_planes[:, i, :],
-                        in0=plain[(b, m0)][:, i, :],
-                        scalar=rows["gain"][:, k : k + 1],
-                        in1=marked[:, i - i0, :],
+                        in0=plain[:, i - i0, :],
+                        scalar=rows[("gain", b)][:, i : i + 1],
+                        in1=marked[:, i, :],
                         op0=ALU.mult,
                         op1=ALU.max,
                     )
@@ -222,9 +263,9 @@ def tile_list_brush_wear_profile_kernel(
                     )
         nc.sync.dma_start(looks[:], offs2)
 
-        nc.vector.tensor_scalar(
-            out=rows["minus_temp"][:], in0=rows["temp"][:], scalar1=-1.0, scalar2=None, op0=ALU.mult
-        )
+        load_rows(nc.gpsimd, "limit", limit, 0)
+        load_rows(nc.gpsimd, "temp", temp, 0)
+        negate_temp(0)
         nc.vector.tensor_copy(out=picked_scales[:], in_=table_scales[:].indirect(picks[:]))
         accs = [[bank(2 * i + c) for c in range(2)] for i in range(PACK)]
         for a in range(K_PASSES):
@@ -238,6 +279,11 @@ def tile_list_brush_wear_profile_kernel(
         load_w1(1, 0)
         load_w1(1, 1)
         load_w1(1, 2)
+        load_rows(nc.sync, "limit", limit, 1)
+        load_rows(nc.sync, "temp", temp, 1)
+        load_rows(nc.sync, "gain", gain, 0)
+        load_rows(nc.sync, "gain", gain, 1)
+        negate_temp(1)
         load_mark(0)
         load_mark(1)
         nc.sync.dma_start(
@@ -249,19 +295,27 @@ def tile_list_brush_wear_profile_kernel(
                 in_=w2_scales[:, 4 * q : 4 * q + 4, :].bitcast(I32).rearrange("a r n -> r a n"),
             )
 
-        for i in range(PACK):
+        for i in range(2):
             clip_scores(0, i, accs[i])
-        for a in range(K_PASSES):
+        for a in range(2):
             round_w1(1, a)
             quantise_w1(1, a)
+        late_accs = []
+        for i in range(PACK):
+            if i >= 2:
+                clip_scores(0, i, accs[i])
+            late_accs.append([bank(2 * i + c) for c in range(2)])
+            for a in range(2):
+                for c in range(2):
+                    first_pass(late_accs[i][c], 1, i, c, a)
+        round_w1(1, 2)
+        quantise_w1(1, 2)
         look(0, 0, M)
 
-        accs = [[bank(2 * i + c) for c in range(2)] for i in range(PACK)]
         for i in range(PACK):
             for c in range(2):
-                for a in range(K_PASSES):
-                    first_pass(accs[i][c], 1, i, c, a)
-            clip_scores(1, i, accs[i])
+                first_pass(late_accs[i][c], 1, i, c, 2)
+            clip_scores(1, i, late_accs[i])
         make_z(0, 0, M)
         for half in range(2):
             look(1, HALF * half, HALF)

@@ -23,7 +23,7 @@ BANK = 512
 K_PASSES = K // K_PASS
 R_PASSES = H // K_PASS
 HALF = M // 2
-VECTOR_SLOTS = ((3, 3, 3), (0, 4, 0))
+VECTOR_SLOTS = ((3, 3, 3), (0, 4, 2))
 
 
 def tile_list_brush_wear_profile_kernel(
@@ -99,7 +99,7 @@ def tile_list_brush_wear_profile_kernel(
             if (b, a) == (1, 1):
                 grouped = keep.tile([P, PACK * K_PASS], BF16, name="w1_late", tag="h2", align_bytes=64)
             elif (b, a) == (1, 2):
-                grouped = keep.tile([P, PACK * K_PASS], BF16, name="w1_last", tag="w1_grouped12", align_bytes=64)
+                grouped = keep.tile([P, PACK * K_PASS], BF16, name="w1_last", tag="h3", align_bytes=64)
             else:
                 grouped = ring.tile([P, PACK * K_PASS], BF16, name="w1_grouped", align_bytes=64)
             dst = grouped[:].rearrange("p (t m j) -> p m t j", t=PACK, j=PACK)
@@ -171,10 +171,9 @@ def tile_list_brush_wear_profile_kernel(
         def look(b, m0, width):
             entries = looks[:, m0 // 16 : (m0 + width) // 16]
             for i0, i1 in slot_groups(b):
-                below_tag = ("w1_raw12" if i0 else "w1_raw10") if b == 0 else "below%d_%d" % (m0, i0)
-                plain_tag = "table%d" % i0 if b == 0 else "plain%d_%d" % (m0, i0)
-                below = keep.tile([P, i1 - i0, width], F32, name="below", tag=below_tag)
-                plain = keep.tile([P, i1 - i0, width], F32, name="plain", tag=plain_tag)
+                tag = ("w1_raw12" if i0 else "w1_raw10") if b == 0 else "found%d_%d" % (m0, i0)
+                both = keep.tile([P, 2, i1 - i0, width], F32, name="found", tag=tag)
+                below, plain = both[:, 0], both[:, 1]
                 for i in range(i0, i1):
                     h = scores[(b, i)]
                     nc.scalar.activation(
@@ -193,7 +192,7 @@ def tile_list_brush_wear_profile_kernel(
         def make_z(b, m0, width):
             if b == 0:
                 z_planes = keep.tile([P, PACK, width], BF16, name="z_planes0", tag="limit1")
-                marked = keep.tile([P, PACK, width], F32, name="marked0", tag="w1_grouped12", align_bytes=64)
+                marked = keep.tile([P, PACK, width], F32, name="marked0", tag="limit0")
             else:
                 z_planes = ring.tile([P, PACK, width], BF16, name="z_planes")
                 marked = ring.tile([P, PACK, width], F32, name="marked")
@@ -201,12 +200,13 @@ def tile_list_brush_wear_profile_kernel(
                 below, plain = found[(b, m0, i0)]
                 if b == 0:
                     for i in range(i0, i1):
-                        nc.gpsimd.tensor_tensor(
+                        engine = nc.gpsimd if i < PACK - 1 else nc.vector
+                        engine.tensor_tensor(
                             out=marked[:, i, :], in0=below[:, i - i0, :], in1=marks[b][:, i, :], op=ALU.mult
                         )
                 else:
                     nc.vector.tensor_tensor(
-                        out=marked[:, i0:i1, :], in0=below[:], in1=marks[b][:, i0:i1, m0 : m0 + width], op=ALU.mult
+                        out=marked[:, i0:i1, :], in0=below, in1=marks[b][:, i0:i1, m0 : m0 + width], op=ALU.mult
                     )
                 for i in range(i0, i1):
                     nc.vector.scalar_tensor_tensor(
@@ -300,21 +300,28 @@ def tile_list_brush_wear_profile_kernel(
         for a in range(2):
             round_w1(1, a)
             quantise_w1(1, a)
-        late_accs = []
-        for i in range(PACK):
-            if i >= 2:
-                clip_scores(0, i, accs[i])
-            late_accs.append([bank(2 * i + c) for c in range(2)])
-            for a in range(2):
+        last = K_PASSES - 1
+        late_accs = {}
+
+        def late_passes(i, passes):
+            if i not in late_accs:
+                late_accs[i] = [bank(2 * i + c) for c in range(2)]
+            for a in passes:
                 for c in range(2):
                     first_pass(late_accs[i][c], 1, i, c, a)
-        round_w1(1, 2)
-        quantise_w1(1, 2)
-        look(0, 0, M)
 
+        for i in range(2):
+            late_passes(i, range(last))
+        clip_scores(0, 2, accs[2])
+        late_passes(2, range(last))
+        round_w1(1, last)
+        quantise_w1(1, last)
+        for i in range(PACK - 1):
+            late_passes(i, [last])
+        clip_scores(0, 3, accs[3])
+        late_passes(3, range(K_PASSES))
+        look(0, 0, M)
         for i in range(PACK):
-            for c in range(2):
-                first_pass(late_accs[i][c], 1, i, c, 2)
             clip_scores(1, i, late_accs[i])
         make_z(0, 0, M)
         for half in range(2):

from contextlib import ExitStack

import concourse.mybir as mybir

K, T, S, H, M, N = 1536, 4096, 1024, 1024, 512, 768
FLOPS = 2 * K * H * S + 2 * H * N * M

F32 = mybir.dt.float32
BF16 = mybir.dt.bfloat16
I32 = mybir.dt.int32
U32 = mybir.dt.uint32
U16 = mybir.dt.uint16
U8 = mybir.dt.uint8
FP8X4 = mybir.dt.float8_e4m3fn_x4
FP4X4 = mybir.dt.float4_e2m1fn_x4
ALU = mybir.AluOpType
ACT = mybir.ActivationFunctionType

P = 128
PACK = 4
K_PASS = P * PACK
BANK = 512
K_PASSES = K // K_PASS
R_PASSES = H // K_PASS
HALF = M // 2
VECTOR_SLOTS = ((3, 3, 3), (0, 4, 2))


def tile_list_brush_wear_profile_kernel(
    tc, tab_words, tab_scales, offs, offs2, w1, limit, temp, mark, gain, w2_words, w2_scales, out
):
    nc = tc.nc
    with ExitStack() as ctx:
        keep = ctx.enter_context(tc.tile_pool(name="keep", bufs=1))
        ring = ctx.enter_context(tc.tile_pool(name="ring", bufs=2))
        psum = ctx.enter_context(tc.psum_pool(name="psum", bufs=1))

        def bank(index):
            return psum.tile([P, BANK], F32, name="bank%d" % index)

        picks = keep.tile([P, S // 16], U16, name="picks")
        looks = keep.tile([P, M // 16], U16, name="looks")
        table = [keep.tile([P, T], I32, name="table%d" % a, tag="table%d" % a) for a in range(K_PASSES)]
        table_scales = keep.tile([P, T], U8, name="table_scales")
        w2_codes = keep.tile([P, R_PASSES, 2 * N], U8, name="w2_codes", align_bytes=64)
        w2_planes = keep.tile([P, R_PASSES, N], U8, name="w2_planes", align_bytes=64)
        marks = {}
        rows = {}
        for name in ("limit", "temp", "gain", "minus_temp", "bias"):
            for b in range(R_PASSES):
                rows[(name, b)] = keep.tile([P, PACK], F32, name="%s%d" % (name, b), tag="%s%d" % (name, b))
        bank_tops = [
            keep.tile([P, 2 * PACK], F32, name="bank_tops%d" % b, tag="bank_tops%d" % b, align_bytes=64)
            for b in range(R_PASSES)
        ]

        nc.vector.memset(table_scales[:].bitcast(I32), 0)
        nc.vector.memset(w2_planes[:].rearrange("p a n -> p (a n)").bitcast(I32), 0)

        def load_rows(queue, name, vec, b):
            src = vec[K_PASS * b : K_PASS * (b + 1)]
            queue.dma_start(out=rows[(name, b)][:], in_=src.rearrange("(p i) -> p i", i=PACK))

        def negate_temp(b):
            nc.vector.tensor_scalar(
                out=rows[("minus_temp", b)][:], in0=rows[("temp", b)][:], scalar1=-1.0, scalar2=None, op0=ALU.mult
            )

        w1_raw = {}

        def load_table(a):
            nc.sync.dma_start(out=table[a][:], in_=tab_words[a].rearrange("p t i -> p (t i)").bitcast(I32))

        def load_w1(b, a):
            raw = keep.tile([P, PACK, K_PASS], F32, name="w1_raw%d%d" % (b, a), tag="w1_raw%d%d" % (b, a))
            src = w1[K_PASS * a : K_PASS * (a + 1), K_PASS * b : K_PASS * (b + 1)]
            src = src.rearrange("(p j) c -> p j c", j=PACK)
            for js in row_pieces(b, a):
                nc.sync.dma_start(out=raw[:, js, :], in_=src[:, js, :])
            w1_raw[(b, a)] = raw

        def row_pieces(b, a):
            if (b, a) == (0, K_PASSES - 1):
                return [slice(0, 2), slice(2, 4)]
            return [slice(0, PACK)]

        def load_mark(b):
            marks[b] = keep.tile([P, PACK, M], F32, name="mark%d" % b, tag="w1_raw0%d" % b)
            src = mark[K_PASS * b : K_PASS * (b + 1), :]
            nc.sync.dma_start(out=marks[b][:], in_=src.rearrange("(p i) m -> p i m", i=PACK))

        picked = [keep.tile([P, S], U32, name="picked%d" % a, align_bytes=64) for a in range(K_PASSES)]
        picked_scales = keep.tile([P, S], U8, name="picked_scales", align_bytes=64)
        w1_codes = {}
        w1_planes = {}
        w1_grouped = {}

        def round_w1(b, a):
            if (b, a) == (1, 1):
                grouped = keep.tile([P, PACK * K_PASS], BF16, name="w1_late", tag="h2", align_bytes=64)
            elif (b, a) == (1, 2):
                grouped = keep.tile([P, PACK * K_PASS], BF16, name="w1_last", tag="h3", align_bytes=64)
            else:
                grouped = ring.tile([P, PACK * K_PASS], BF16, name="w1_grouped", align_bytes=64)
            dst = grouped[:].rearrange("p (t m j) -> p m t j", t=PACK, j=PACK)
            src = w1_raw[(b, a)][:].rearrange("p j (m t) -> p m t j", t=PACK)
            cut = VECTOR_SLOTS[b][a]
            for js in row_pieces(b, a):
                if cut:
                    nc.vector.tensor_copy(out=dst[:, :, :cut, js], in_=src[:, :, :cut, js])
                if cut < PACK:
                    nc.scalar.copy(out=dst[:, :, cut:, js], in_=src[:, :, cut:, js])
            w1_grouped[(b, a)] = grouped

        def quantise_w1(b, a):
            codes = keep.tile([P, K_PASS], U32, name="w1_codes%d%d" % (b, a), align_bytes=64)
            plane = keep.tile([P, K_PASS], U8, name="w1_plane%d%d" % (b, a), align_bytes=64)
            width = P if (b, a) == (0, K_PASSES - 1) else K_PASS
            for c0 in range(0, K_PASS, width):
                nc.vector.quantize_mx(
                    out=codes[:, c0 : c0 + width].bitcast(FP8X4),
                    scales=plane[:, c0 : c0 + width],
                    in_=w1_grouped[(b, a)][:, PACK * c0 : PACK * (c0 + width)],
                )
            w1_codes[(b, a)] = codes
            w1_planes[(b, a)] = plane

        def first_pass(acc, b, i, c, a):
            stat = slice(P * i, P * (i + 1))
            cols = slice(BANK * c, BANK * (c + 1))
            nc.tensor.matmul_mx(
                out=acc[:],
                lhsT=w1_codes[(b, a)][:, stat].bitcast(FP8X4),
                lhsT_scale=w1_planes[(b, a)][:, stat],
                rhs=picked[a][:, cols].bitcast(FP8X4),
                rhs_scale=picked_scales[4 * a :, cols],
                start=(a == 0),
                stop=(a == K_PASSES - 1),
            )

        scores = {}

        def clip_scores(b, i, accs):
            k = PACK * b + i
            h = keep.tile([P, S], F32, name="h%d" % k, tag="h%d" % k, align_bytes=64)
            for c in range(2):
                nc.vector.tensor_scalar(
                    out=h[:, BANK * c : BANK * (c + 1)],
                    in0=accs[c][:],
                    scalar1=rows[("limit", b)][:, i : i + 1],
                    scalar2=None,
                    op0=ALU.min,
                    op1=ALU.max,
                    accum_out=bank_tops[b][:, 2 * i + c : 2 * i + c + 1],
                )
            nc.gpsimd.tensor_scalar(
                out=rows[("bias", b)][:, i : i + 1],
                in0=bank_tops[b][:, 2 * i : 2 * i + 1],
                scalar1=bank_tops[b][:, 2 * i + 1 : 2 * i + 2],
                scalar2=rows[("minus_temp", b)][:, i : i + 1],
                op0=ALU.max,
                op1=ALU.mult,
            )
            scores[(b, i)] = h

        found = {}

        def slot_groups(b):
            return [(0, 1), (1, PACK)] if b == 0 else [(0, 2), (2, PACK)]

        def look(b, m0, width):
            entries = looks[:, m0 // 16 : (m0 + width) // 16]
            for i0, i1 in slot_groups(b):
                tag = ("w1_raw12" if i0 else "w1_raw10") if b == 0 else "found%d_%d" % (m0, i0)
                both = keep.tile([P, 2, i1 - i0, width], F32, name="found", tag=tag)
                below, plain = both[:, 0], both[:, 1]
                for i in range(i0, i1):
                    h = scores[(b, i)]
                    nc.scalar.activation(
                        out=below[:, i - i0, :],
                        in_=h[:].indirect(entries),
                        func=ACT.Exp,
                        bias=rows[("bias", b)][:, i : i + 1],
                        scale=rows[("temp", b)][:, i : i + 1],
                    )
                    nc.scalar.activation(out=plain[:, i - i0, :], in_=h[:].indirect(entries), func=ACT.Copy)
                found[(b, m0, i0)] = (below, plain)

        z_codes = [keep.tile([P, M], U32, name="z_codes%d" % b, align_bytes=64) for b in range(R_PASSES)]
        z_scales = [keep.tile([P, M], U8, name="z_scales%d" % b, align_bytes=64) for b in range(R_PASSES)]

        def make_z(b, m0, width):
            if b == 0:
                z_planes = keep.tile([P, PACK, width], BF16, name="z_planes0", tag="limit1")
                marked = keep.tile([P, PACK, width], F32, name="marked0", tag="limit0")
            else:
                z_planes = ring.tile([P, PACK, width], BF16, name="z_planes")
                marked = ring.tile([P, PACK, width], F32, name="marked")
            for i0, i1 in slot_groups(b):
                below, plain = found[(b, m0, i0)]
                if b == 0:
                    for i in range(i0, i1):
                        engine = nc.gpsimd if i < PACK - 1 else nc.vector
                        engine.tensor_tensor(
                            out=marked[:, i, :], in0=below[:, i - i0, :], in1=marks[b][:, i, :], op=ALU.mult
                        )
                else:
                    nc.vector.tensor_tensor(
                        out=marked[:, i0:i1, :], in0=below, in1=marks[b][:, i0:i1, m0 : m0 + width], op=ALU.mult
                    )
                for i in range(i0, i1):
                    nc.vector.scalar_tensor_tensor(
                        out=z_planes[:, i, :],
                        in0=plain[:, i - i0, :],
                        scalar=rows[("gain", b)][:, i : i + 1],
                        in1=marked[:, i, :],
                        op0=ALU.mult,
                        op1=ALU.max,
                    )
            grouped = ring.tile([P, PACK * width], BF16, name="z_grouped", align_bytes=64)
            nc.vector.tensor_copy(
                out=grouped[:].rearrange("p (c u i) -> p c i u", u=4, i=PACK),
                in_=z_planes[:].rearrange("p i (c u) -> p c i u", u=4),
            )
            nc.vector.quantize_mx(
                out=z_codes[b][:, m0 : m0 + width].bitcast(FP8X4),
                scales=z_scales[b][:, m0 : m0 + width],
                in_=grouped[:],
            )

        def second_pass(acc, pair, m0, b):
            cols = slice(m0, m0 + HALF)
            for u in range(2):
                n0 = P * (2 * pair + u)
                nc.tensor.matmul_mx(
                    out=acc[:, HALF * u : HALF * (u + 1)],
                    lhsT=w2_codes[:, b, 2 * n0 : 2 * (n0 + P)].bitcast(FP4X4),
                    lhsT_scale=w2_planes[:, b, n0 : n0 + P],
                    rhs=z_codes[b][:, cols].bitcast(FP8X4),
                    rhs_scale=z_scales[b][:, cols],
                    start=(b == 0 and u == 0),
                    stop=(b == R_PASSES - 1 and u == 1),
                )

        def finish(acc, pair, m0):
            result = results[pair][:, m0 // HALF, :]
            nc.scalar.activation(out=result, in_=acc[:], func=ACT.Tanh)
            dst = out[2 * P * pair : 2 * P * (pair + 1), m0 : m0 + HALF]
            nc.sync.dma_start(
                out=dst.rearrange("(u p) m -> p u m", p=P),
                in_=result.rearrange("p (u m) -> p u m", u=2),
            )

        nc.sync.dma_start(picks[:], offs)
        for a in range(K_PASSES):
            load_table(a)
            load_w1(0, a)
            if a == 0:
                for q in range(4):
                    nc.sync.dma_start(
                        out=table_scales[32 * q : 32 * q + 4 * K_PASSES, :].bitcast(I32),
                        in_=tab_scales[:, 4 * q : 4 * q + 4, :].bitcast(I32),
                    )
        nc.sync.dma_start(looks[:], offs2)

        load_rows(nc.gpsimd, "limit", limit, 0)
        load_rows(nc.gpsimd, "temp", temp, 0)
        negate_temp(0)
        nc.vector.tensor_copy(out=picked_scales[:], in_=table_scales[:].indirect(picks[:]))
        accs = [[bank(2 * i + c) for c in range(2)] for i in range(PACK)]
        for a in range(K_PASSES):
            nc.vector.tensor_copy(out=picked[a][:], in_=table[a][:].bitcast(U32).indirect(picks[:]))
            round_w1(0, a)
            quantise_w1(0, a)
            for i in range(PACK):
                for c in range(2):
                    first_pass(accs[i][c], 0, i, c, a)

        load_w1(1, 0)
        load_w1(1, 1)
        load_w1(1, 2)
        load_rows(nc.sync, "limit", limit, 1)
        load_rows(nc.sync, "temp", temp, 1)
        load_rows(nc.sync, "gain", gain, 0)
        load_rows(nc.sync, "gain", gain, 1)
        negate_temp(1)
        load_mark(0)
        load_mark(1)
        nc.sync.dma_start(
            out=w2_codes[:].bitcast(I32), in_=w2_words.bitcast(I32).rearrange("a p n -> p a n")
        )
        for q in range(4):
            nc.sync.dma_start(
                out=w2_planes[32 * q : 32 * q + 4].bitcast(I32),
                in_=w2_scales[:, 4 * q : 4 * q + 4, :].bitcast(I32).rearrange("a r n -> r a n"),
            )

        for i in range(2):
            clip_scores(0, i, accs[i])
        for a in range(2):
            round_w1(1, a)
            quantise_w1(1, a)
        last = K_PASSES - 1
        late_accs = {}

        def late_passes(i, passes):
            if i not in late_accs:
                late_accs[i] = [bank(2 * i + c) for c in range(2)]
            for a in passes:
                for c in range(2):
                    first_pass(late_accs[i][c], 1, i, c, a)

        for i in range(2):
            late_passes(i, range(last))
        clip_scores(0, 2, accs[2])
        late_passes(2, range(last))
        round_w1(1, last)
        quantise_w1(1, last)
        for i in range(PACK - 1):
            late_passes(i, [last])
        clip_scores(0, 3, accs[3])
        late_passes(3, range(K_PASSES))
        look(0, 0, M)
        for i in range(PACK):
            clip_scores(1, i, late_accs[i])
        make_z(0, 0, M)
        for half in range(2):
            look(1, HALF * half, HALF)

        results = [keep.tile([P, 2, BANK], F32, name="result%d" % pair, tag="table%d" % pair) for pair in range(3)]
        for half in range(2):
            outs = [bank(3 * half + pair) for pair in range(3)]
            for pair in range(3):
                second_pass(outs[pair], pair, HALF * half, 0)
            make_z(1, HALF * half, HALF)
            for pair in range(3):
                second_pass(outs[pair], pair, HALF * half, 1)
                finish(outs[pair], pair, HALF * half)
